import numpy as np
import ml_dtypes


def mxq(x, axis, fmt="e4m3"):
    dtype, down = {"e4m3": (ml_dtypes.float8_e4m3fn, 7), "e5m2": (ml_dtypes.float8_e5m2, 14)}[fmt]
    v = np.moveaxis(np.asarray(x, np.float32).astype(ml_dtypes.bfloat16).astype(np.float64), axis, -1)
    blocks = v.reshape(v.shape[:-1] + (-1, 32))
    amax = np.abs(blocks).max(-1, keepdims=True)
    byte = np.maximum(np.where(amax > 0, np.frexp(amax)[1] - 1 + 127, 0) - down, 1)
    scale = np.exp2(byte - 127.0)
    codes = (blocks / scale).astype(np.float32).astype(dtype).astype(np.float64)
    return np.moveaxis((codes * scale).reshape(v.shape), -1, axis)


WIDE = False


def mx_kscale(k):
    if not WIDE:
        return np.ones(k)
    levels = np.array([10, -10, 5, -5, 0])
    if k % 512:
        return np.exp2(np.random.permutation(np.resize(levels, k // 32))).repeat(32)
    a = np.empty((k // 512, 16))
    for p in range(k // 512):
        a[p, :8] = np.random.permutation(np.resize(levels, 8))
        for g in range(8):
            far = levels[np.abs(levels - a[p, g]) >= 10]
            a[p, g + 8] = far[np.random.randint(len(far))]
    return np.exp2(a.ravel()).repeat(32)


def f64(x):
    return np.asarray(x).astype(np.float64)


def striped(idx):
    return np.tile(idx.reshape(-1, 16).T, (8, 1)).astype(np.uint16)


def unstriped(offs):
    return offs[:16].T.reshape(-1).astype(np.int64)


def striped8(idx):
    return np.concatenate([x.reshape(-1, 16).T for x in idx]).astype(np.uint16)


def runs(offs, k):
    lists = np.stack([offs[16 * r : 16 * r + 16].T.reshape(-1) for r in range(8)]).astype(np.int64)
    return lists[np.arange(k) % 512 // 64]


def pack_weight(w):
    k, n = w.shape
    w = f64(np.asarray(w, np.float32).astype(ml_dtypes.bfloat16)).reshape(k // 32, 32, n)
    amax = np.abs(w).max(1)
    byte = np.clip(np.where(amax > 0, np.frexp(amax)[1] - 1 + 127 - 7, 1), 1, 254)
    scaled = (w * np.exp2(127.0 - byte)[:, None, :]).reshape(k, n).astype(np.float32)
    words = np.ascontiguousarray(scaled.reshape(k // 512, 128, 4, n).transpose(0, 1, 3, 2)).astype(ml_dtypes.float8_e4m3fn).view(np.uint8)
    return words, np.ascontiguousarray(byte.astype(np.uint8).reshape(k // 512, 16, n))


def unpack_weight(words, scales):
    g, p, n, _ = words.shape
    vals = np.ascontiguousarray(words).view(ml_dtypes.float8_e4m3fn).astype(np.float64) * np.repeat(np.exp2(scales.astype(np.float64) - 127.0), 8, axis=1)[..., None]
    return vals.transpose(0, 1, 3, 2).reshape(g * 512, n)


def sigmoid(v):
    return 1.0 / (1.0 + np.exp(-np.maximum(v, -700.0)))

def planes(y):
    n, m = y.shape
    v = y.astype(np.float32).astype(ml_dtypes.bfloat16).astype(np.float64).reshape(n // 32, 32, m)
    top = np.abs(v).max(1)
    byte = np.clip(np.where(top > 0, np.frexp(top)[1] - 1 + 127 - 7, 1), 1, 254)
    codes = (v * np.exp2(127.0 - byte)[:, None, :]).reshape(n, m).astype(np.float32).astype(ml_dtypes.float8_e4m3fn).view(np.uint8)
    words = codes.reshape(n // 512, 128, 4, m).transpose(0, 1, 3, 2)
    return np.ascontiguousarray(words), np.ascontiguousarray(byte.astype(np.uint8).reshape(n // 512, 16, m))


K, T, S, N, H, G = 512, 2048, 512, 512, 512, 2048


def setup_inputs():
    n = np.random.standard_normal
    s = mx_kscale(K)[:, None]
    u = mx_kscale(S)
    packed_xT = pack_weight(n((K, T)) * s)
    packed_w1 = pack_weight(n((K, H)) / np.sqrt(K) / s)
    packed_w2 = pack_weight(n((H, N)) / np.sqrt(H) / u[:, None])
    packed_dT = pack_weight(n((K, G)) / s)
    return {
        "x_words": packed_xT[0],
        "x_scales": packed_xT[1],
        "w1_words": packed_w1[0],
        "w1_scales": packed_w1[1],
        "gn": (np.random.uniform(0.5, 1.5, (H, 1)) * u[:, None]).astype(np.float32),
        "w2_words": packed_w2[0],
        "w2_scales": packed_w2[1],
        "d_words": packed_dT[0],
        "d_scales": packed_dT[1],
        "offs": striped(np.random.permutation(T)[:S]),
        "n1": striped8(np.stack([np.random.permutation(S) for _ in range(8)])),
        "two": striped(np.random.permutation(T)[:S]),
        "k1": striped8(np.random.randint(0, G, (8, H))),
        "n2": striped8(np.stack([np.random.permutation(S) for _ in range(8)])),
        "n3": striped8(np.stack([np.random.permutation(S) for _ in range(8)])),
    }


def reference(x_words, x_scales, w1_words, w1_scales, gn, w2_words, w2_scales, d_words, d_scales, offs, n1, two, k1, n2, n3):
    xq = unpack_weight(x_words, x_scales)[:, unstriped(offs)]
    y = unpack_weight(w1_words, w1_scales).T @ xq
    z = f64(gn) * (y * (sigmoid(y[np.arange(H)[:, None], runs(n1, H)])))
    a = unpack_weight(w2_words, w2_scales).T @ mxq(z, 0, "e4m3")
    d_k1 = unpack_weight(d_words, d_scales)[np.arange(K)[:, None], runs(k1, K)]
    x_two = unpack_weight(x_words, x_scales)[:, unstriped(two)]
    b = 0.0625 * (d_k1.T @ x_two)
    out_0 = (a + a[np.arange(N)[:, None], runs(n2, N)]) * (sigmoid(b + b[np.arange(H)[:, None], runs(n3, H)]))
    return (out_0,) + planes(out_0)

@@ -1,0 +1,240 @@
+from contextlib import ExitStack
+
+import concourse.mybir as mybir
+from concourse.masks import make_identity
+
+F32 = mybir.dt.float32
+BF16 = mybir.dt.bfloat16
+I32 = mybir.dt.int32
+U32 = mybir.dt.uint32
+U16 = mybir.dt.uint16
+U8 = mybir.dt.uint8
+FP8X4 = mybir.dt.float8_e4m3fn_x4
+ACT = mybir.ActivationFunctionType
+MULT = mybir.AluOpType.mult
+ADD = mybir.AluOpType.add
+
+P = 128
+PACK = 4
+T = 2048
+S = 512
+HALF = S // 2
+LIST_COLS = S // 16
+FLOPS = 3 * 2 * 512 * 512 * 512
+
+
+def tile_picked_cdjointriebgate_none_po_kernel(
+    tc, x_words, x_scales, w1_words, w1_scales, gn, w2_words, w2_scales, d_words, d_scales,
+    offs, n1, two, k1, n2, n3, out_0, out_1, out_2,
+):
+    nc = tc.nc
+
+    def words_of(dram):
+        return dram[0].rearrange("p n r -> p (n r)").bitcast(I32)
+
+    def half_cols(h):
+        return slice(h * HALF, (h + 1) * HALF)
+
+    def half_list(lst, h):
+        return lst[:, h * LIST_COLS // 2 : (h + 1) * LIST_COLS // 2]
+
+    def block(t):
+        return slice(t * P, (t + 1) * P)
+
+    with ExitStack() as ctx:
+        keep = ctx.enter_context(tc.tile_pool(name="keep", bufs=1))
+        turns = ctx.enter_context(tc.tile_pool(name="turns", bufs=1))
+        psum = ctx.enter_context(tc.psum_pool(name="psum", bufs=1))
+
+        def sb(name, shape, dtype):
+            return keep.tile(shape, dtype, name=name, align_bytes=64)
+
+        def load_list(name, dram):
+            lst = keep.tile([P, LIST_COLS], U16, name=name)
+            nc.sync.dma_start(lst[:], dram)
+            return lst
+
+        def placed(name, shape, dtype, offset):
+            return turns.tile(shape, dtype, name=name, offset=offset, align_bytes=64)
+
+        def load_plane(plane, dram, clear, queues):
+            clear.memset(plane[:].bitcast(I32), 0)
+            for q, queue in enumerate(queues):
+                queue.dma_start(plane[32 * q : 32 * q + 4, :].bitcast(I32), dram[0, 4 * q : 4 * q + 4, :].bitcast(I32))
+
+        def deal(name, src, dtype):
+            dst = sb(name, [P, S], dtype)
+            nc.vector.tensor_copy(out=dst[:].rearrange("p (t m) -> p t m", t=PACK), in_=src.rearrange("p (m t) -> p t m", t=PACK))
+            return dst
+
+        l_offs = load_list("l_offs", offs)
+        l_two = load_list("l_two", two)
+        l_k1 = load_list("l_k1", k1)
+        l_n1 = load_list("l_n1", n1)
+        l_n3 = load_list("l_n3", n3)
+        l_n2 = load_list("l_n2", n2)
+        w1w = placed("w1w", [P, S], I32, 1024)
+        nc.sync.dma_start(w1w[:], words_of(w1_words))
+        xw = sb("xw", [P, T], I32)
+        nc.sync.dma_start(xw[:], words_of(x_words))
+        xs = sb("xs", [P, T], U8)
+        load_plane(xs, x_scales, nc.vector, [nc.scalar] * 4)
+        w1s = placed("w1s", [P, S], U8, 12288)
+        load_plane(w1s, w1_scales, nc.gpsimd, [nc.gpsimd, nc.gpsimd, nc.scalar, nc.scalar])
+        ident = sb("ident", [P, P], F32)
+        make_identity(nc, ident[:])
+        d_plane = sb("d_plane", [P, S], U8)
+        nc.vector.memset(d_plane[:].bitcast(I32), 0)
+
+        w1_codes = deal("w1_codes", w1w[:].bitcast(U32), U32)
+        dw = placed("dw", [P, T], I32, 2048)
+        nc.sync.dma_start(dw[:], words_of(d_words))
+        ds = placed("ds", [P, T], U8, 0)
+        nc.gpsimd.memset(ds[:].bitcast(I32), 0)
+        for r in range(2):
+            nc.sync.dma_start(ds[r:P:16, :].bitcast(I32), d_scales[0, r:16:2, :].bitcast(I32))
+        xq_s = sb("xq_s", [P, S], U8)
+        nc.vector.tensor_copy(xq_s[:], xs[:].indirect(l_offs[:]))
+        w1_plane = deal("w1_plane", w1s[:], U8)
+        gain = placed("gain", [P, PACK], F32, 12288 + 64)
+        nc.sync.dma_start(gain[:], gn.rearrange("(p t) o -> p (t o)", t=PACK))
+        w2w = placed("w2w", [P, S], I32, 12288 + 64 - 2048)
+        nc.sync.dma_start(w2w[:], words_of(w2_words))
+        w2s = placed("w2s", [P, S], U8, 12288 + 128)
+        load_plane(w2s, w2_scales, nc.gpsimd, [nc.sync] * 4)
+        xq = sb("xq", [P, S], U32)
+        y_banks = {}
+        sig_y = [sb("sig_y%d" % t, [P, S], F32) for t in range(PACK)]
+        for h in range(2):
+            nc.vector.tensor_copy(xq[:, half_cols(h)], xw[:].bitcast(U32).indirect(half_list(l_offs, h)))
+            for pair in range(2):
+                bank = psum.tile([P, 2, HALF], F32, name="y%d%d" % (h, pair), tag="main%d%d" % (h, pair))
+                y_banks[h, pair] = bank
+                for i in range(2):
+                    t = 2 * pair + i
+                    nc.tensor.matmul_mx(
+                        out=bank[:, i, :], lhsT=w1_codes[:, block(t)].bitcast(FP8X4), lhsT_scale=w1_plane[:, block(t)],
+                        rhs=xq[:, half_cols(h)].bitcast(FP8X4), rhs_scale=xq_s[:, half_cols(h)], start=True, stop=True,
+                    )
+                for i in range(2):
+                    nc.scalar.activation(sig_y[2 * pair + i][:, half_cols(h)], bank[:, i, :], ACT.Sigmoid)
+
+        x2_s = sb("x2_s", [P, S], U8)
+        nc.vector.tensor_copy(x2_s[:], xs[:].indirect(l_two[:]))
+        dk_s = sb("dk_s", [P, S], U8)
+        nc.vector.tensor_copy(dk_s[:], ds[:].indirect(l_k1[:]))
+        dk_s_dealt = deal("dk_s_dealt", dk_s[:], U8)
+        for odd in range(2):
+            for r in range(2):
+                nc.sync.dma_start(d_plane[2 * odd + r : P : 32, :].bitcast(I32), dk_s_dealt[16 * odd + r : P : 32, :].bitcast(I32))
+        x2 = sb("x2", [P, S], U32)
+        nc.vector.tensor_copy(x2[:], xw[:].bitcast(U32).indirect(l_two[:]))
+        dk = sb("dk", [P, S], U32)
+        nc.vector.tensor_copy(dk[:], dw[:].bitcast(U32).indirect(l_k1[:]))
+        d_codes = deal("d_codes", dk[:], U32)
+        w2_codes = deal("w2_codes", w2w[:].bitcast(U32), U32)
+        w2_plane = deal("w2_plane", w2s[:], U8)
+
+        z_codes = sb("z_codes", [P, S], U32)
+        z_plane = sb("z_plane", [P, S], U8)
+        a_rows = [sb("a_rows%d" % t, [P, S], F32) for t in range(PACK)]
+        a_banks = {}
+
+        def gate_half(h):
+            z = sb("z%d" % h, [P, PACK, HALF], BF16)
+            for t in range(PACK):
+                g = sb("gy%d%d" % (h, t), [P, HALF], F32)
+                nc.scalar.activation(g[:], sig_y[t][:].indirect(half_list(l_n1, h)), ACT.Copy)
+                nc.vector.scalar_tensor_tensor(
+                    out=z[:, t, :], in0=y_banks[h, t // 2][:, t % 2, :], scalar=gain[:, t : t + 1], in1=g[:], op0=MULT, op1=MULT,
+                )
+            woven = sb("zw%d" % h, [P, HALF, PACK], BF16)
+            nc.vector.tensor_copy(
+                out=woven[:].rearrange("p (c i) t -> p c t i", i=4), in_=z[:].rearrange("p t (c i) -> p c t i", i=4),
+            )
+            nc.vector.quantize_mx(
+                out=z_codes[:, half_cols(h)].bitcast(FP8X4), scales=z_plane[:, half_cols(h)], in_=woven[:].rearrange("p c t -> p (c t)"),
+            )
+            for pair in range(2):
+                bank = psum.tile([P, 2, HALF], F32, name="a%d%d" % (h, pair), tag="main%d%d" % (h, pair))
+                a_banks[h, pair] = bank
+                for i in range(2):
+                    t = 2 * pair + i
+                    nc.tensor.matmul_mx(
+                        out=bank[:, i, :], lhsT=w2_codes[:, block(t)].bitcast(FP8X4), lhsT_scale=w2_plane[:, block(t)],
+                        rhs=z_codes[:, half_cols(h)].bitcast(FP8X4), rhs_scale=z_plane[:, half_cols(h)], start=True, stop=True,
+                    )
+
+        def rows_of_a(h):
+            for t in range(PACK):
+                nc.scalar.copy(a_rows[t][:, half_cols(h)], a_banks[h, t // 2][:, t % 2, :])
+
+        gate_half(0)
+        gate_half(1)
+
+        b_rows = [sb("b_rows%d" % t, [P, S], F32) for t in range(PACK)]
+        for t in range(PACK):
+            bank = psum.tile([P, S], F32, name="b%d" % t, tag="side%d" % t)
+            nc.tensor.matmul_mx(
+                out=bank[:], lhsT=d_codes[:, block(t)].bitcast(FP8X4), lhsT_scale=d_plane[:, block(t)],
+                rhs=x2[:].bitcast(FP8X4), rhs_scale=x2_s[:], start=True, stop=True,
+            )
+            nc.scalar.copy(b_rows[t][:], bank[:])
+
+        o_codes = sb("o_codes", [P, S], U32)
+        o_plane = sb("o_plane", [P, S], U8)
+        out_rows = out_0.rearrange("(p t) j -> p t j", t=PACK)
+
+        def fetch_b(h, pair):
+            gb = sb("gb%d%d" % (h, pair), [P, 2, HALF], F32)
+            for i in range(2):
+                window = b_rows[2 * pair + i][:].indirect(half_list(l_n3, h))
+                if (h, pair) == (0, 0):
+                    nc.scalar.activation(gb[:, i, :], window, ACT.Copy)
+                else:
+                    nc.vector.tensor_copy(gb[:, i, :], window)
+            return gb
+
+        def gate_of_b(h, pair, gb):
+            tag = "side%d" % (2 * h + pair)
+            total = psum.tile([P, 4, P], F32, name="bsum%d%d" % (h, pair), tag=tag)
+            for i in range(2):
+                for jb in range(2):
+                    cols = slice(h * HALF + jb * P, h * HALF + (jb + 1) * P)
+                    nc.tensor.matmul(total[:, 2 * i + jb, :], b_rows[2 * pair + i][:, cols], ident[:], is_transpose=True, start=True, stop=False)
+                    nc.tensor.matmul(total[:, 2 * i + jb, :], gb[:, i, block(jb)], ident[:], is_transpose=True, start=False, stop=True)
+            turned = sb("turned%d%d" % (h, pair), [P, 4, P], F32)
+            nc.scalar.activation(turned[:], total[:], ACT.Sigmoid, scale=0.0625)
+            gate = psum.tile([P, 4, P], F32, name="gate%d%d" % (h, pair), tag=tag)
+            for k in range(4):
+                nc.tensor.transpose(gate[:, k, :], turned[:, k, :], ident[:])
+            return gate
+
+        fetched = {(h, pair): fetch_b(h, pair) for h in range(2) for pair in range(2)}
+        rows_of_a(0)
+        rows_of_a(1)
+        for h in range(2):
+            res = sb("res%d" % h, [P, PACK, HALF], F32)
+            gates = [gate_of_b(h, pair, fetched[h, pair]) for pair in range(2)]
+            for pair in range(2):
+                ga = sb("ga%d%d" % (h, pair), [P, 2, HALF], F32)
+                for i in range(2):
+                    nc.scalar.activation(ga[:, i, :], a_rows[2 * pair + i][:].indirect(half_list(l_n2, h)), ACT.Copy)
+                both = sb("both%d%d" % (h, pair), [P, 2, HALF], F32)
+                nc.vector.tensor_tensor(both[:], a_banks[h, pair][:], ga[:], ADD)
+                nc.vector.tensor_tensor(
+                    res[:, 2 * pair : 2 * pair + 2, :].rearrange("p i c -> p (i c)"), both[:].rearrange("p i c -> p (i c)"),
+                    gates[pair][:].rearrange("p k c -> p (k c)"), MULT,
+                )
+                nc.sync.dma_start(out_rows[:, 2 * pair : 2 * pair + 2, half_cols(h)], res[:, 2 * pair : 2 * pair + 2, :])
+            woven = sb("ow%d" % h, [P, HALF, PACK], BF16)
+            nc.vector.tensor_copy(
+                out=woven[:].rearrange("p (c i) t -> p c t i", i=4), in_=res[:].rearrange("p t (c i) -> p c t i", i=4),
+            )
+            nc.vector.quantize_mx(
+                out=o_codes[:, half_cols(h)].bitcast(FP8X4), scales=o_plane[:, half_cols(h)], in_=woven[:].rearrange("p c t -> p (c t)"),
+            )
+            nc.sync.dma_start(words_of(out_1)[:, half_cols(h)], o_codes[:, half_cols(h)].bitcast(I32))
+        for q in range(4):
+            queue = nc.scalar if q % 2 else nc.sync
+            queue.dma_start(out_2[0, 4 * q : 4 * q + 4, :].bitcast(I32), o_plane[32 * q : 32 * q + 4, :].bitcast(I32))

@@ -46,8 +46,8 @@ def tile_picked_cdjointriebgate_none_po_kernel(
         turns = ctx.enter_context(tc.tile_pool(name="turns", bufs=1))
         psum = ctx.enter_context(tc.psum_pool(name="psum", bufs=1))
 
-        def sb(name, shape, dtype):
-            return keep.tile(shape, dtype, name=name, align_bytes=64)
+        def sb(name, shape, dtype, tag=None):
+            return keep.tile(shape, dtype, name=name, tag=tag or name, align_bytes=64)
 
         def load_list(name, dram):
             lst = keep.tile([P, LIST_COLS], U16, name=name)
@@ -57,14 +57,15 @@ def tile_picked_cdjointriebgate_none_po_kernel(
         def placed(name, shape, dtype, offset):
             return turns.tile(shape, dtype, name=name, offset=offset, align_bytes=64)
 
-        def load_plane(plane, dram, clear, queues):
+        def load_plane(plane, dram, clear, first_queue=nc.sync):
             clear.memset(plane[:].bitcast(I32), 0)
-            for q, queue in enumerate(queues):
+            for q in range(4):
+                queue = nc.sync if q else first_queue
                 queue.dma_start(plane[32 * q : 32 * q + 4, :].bitcast(I32), dram[0, 4 * q : 4 * q + 4, :].bitcast(I32))
 
-        def deal(name, src, dtype):
+        def deal(name, src, dtype, engine=nc.vector):
             dst = sb(name, [P, S], dtype)
-            nc.vector.tensor_copy(out=dst[:].rearrange("p (t m) -> p t m", t=PACK), in_=src.rearrange("p (m t) -> p t m", t=PACK))
+            engine.tensor_copy(out=dst[:].rearrange("p (t m) -> p t m", t=PACK), in_=src.rearrange("p (m t) -> p t m", t=PACK))
             return dst
 
         l_offs = load_list("l_offs", offs)
@@ -73,39 +74,36 @@ def tile_picked_cdjointriebgate_none_po_kernel(
         l_n1 = load_list("l_n1", n1)
         l_n3 = load_list("l_n3", n3)
         l_n2 = load_list("l_n2", n2)
-        w1w = placed("w1w", [P, S], I32, 1024)
+        w1w = placed("w1w", [P, S], I32, 4 * T - 64)
         nc.sync.dma_start(w1w[:], words_of(w1_words))
         xw = sb("xw", [P, T], I32)
         nc.sync.dma_start(xw[:], words_of(x_words))
-        xs = sb("xs", [P, T], U8)
-        load_plane(xs, x_scales, nc.vector, [nc.scalar] * 4)
-        w1s = placed("w1s", [P, S], U8, 12288)
-        load_plane(w1s, w1_scales, nc.gpsimd, [nc.gpsimd, nc.gpsimd, nc.scalar, nc.scalar])
+        w1s = sb("w1s", [P, S], U8)
+        load_plane(w1s, w1_scales, nc.gpsimd, nc.gpsimd)
+        xs = sb("xs", [P, T], U8, "xs")
+        load_plane(xs, x_scales, nc.vector)
         ident = sb("ident", [P, P], F32)
         make_identity(nc, ident[:])
-        d_plane = sb("d_plane", [P, S], U8)
-        nc.vector.memset(d_plane[:].bitcast(I32), 0)
+        ds = sb("ds", [P, T], U8)
+        nc.vector.memset(ds[:].bitcast(I32), 0)
+        nc.sync.dma_start(ds[0:P:8, :].bitcast(I32), d_scales[0].bitcast(I32))
 
         w1_codes = deal("w1_codes", w1w[:].bitcast(U32), U32)
-        dw = placed("dw", [P, T], I32, 2048)
+        dw = placed("dw", [P, T], I32, 0)
         nc.sync.dma_start(dw[:], words_of(d_words))
-        ds = placed("ds", [P, T], U8, 0)
-        nc.gpsimd.memset(ds[:].bitcast(I32), 0)
-        for r in range(2):
-            nc.sync.dma_start(ds[r:P:16, :].bitcast(I32), d_scales[0, r:16:2, :].bitcast(I32))
-        xq_s = sb("xq_s", [P, S], U8)
-        nc.vector.tensor_copy(xq_s[:], xs[:].indirect(l_offs[:]))
-        w1_plane = deal("w1_plane", w1s[:], U8)
-        gain = placed("gain", [P, PACK], F32, 12288 + 64)
+        gain = placed("gain", [P, PACK], F32, 4 * T)
         nc.sync.dma_start(gain[:], gn.rearrange("(p t) o -> p (t o)", t=PACK))
-        w2w = placed("w2w", [P, S], I32, 12288 + 64 - 2048)
+        w2w = placed("w2w", [P, S], I32, 4 * T + 64 + S)
         nc.sync.dma_start(w2w[:], words_of(w2_words))
-        w2s = placed("w2s", [P, S], U8, 12288 + 128)
-        load_plane(w2s, w2_scales, nc.gpsimd, [nc.sync] * 4)
+        w2s = placed("w2s", [P, S], U8, 4 * T + 64)
+        load_plane(w2s, w2_scales, nc.gpsimd)
+        w1_plane = deal("w1_plane", w1s[:], U8)
+        xq_s = sb("xq_s", [P, S], U8)
         xq = sb("xq", [P, S], U32)
         y_banks = {}
         sig_y = [sb("sig_y%d" % t, [P, S], F32) for t in range(PACK)]
         for h in range(2):
+            nc.vector.tensor_copy(xq_s[:, half_cols(h)], xs[:].indirect(half_list(l_offs, h)))
             nc.vector.tensor_copy(xq[:, half_cols(h)], xw[:].bitcast(U32).indirect(half_list(l_offs, h)))
             for pair in range(2):
                 bank = psum.tile([P, 2, HALF], F32, name="y%d%d" % (h, pair), tag="main%d%d" % (h, pair))
@@ -119,21 +117,29 @@ def tile_picked_cdjointriebgate_none_po_kernel(
                 for i in range(2):
                     nc.scalar.activation(sig_y[2 * pair + i][:, half_cols(h)], bank[:, i, :], ACT.Sigmoid)
 
-        x2_s = sb("x2_s", [P, S], U8)
-        nc.vector.tensor_copy(x2_s[:], xs[:].indirect(l_two[:]))
         dk_s = sb("dk_s", [P, S], U8)
         nc.vector.tensor_copy(dk_s[:], ds[:].indirect(l_k1[:]))
-        dk_s_dealt = deal("dk_s_dealt", dk_s[:], U8)
-        for odd in range(2):
-            for r in range(2):
-                nc.sync.dma_start(d_plane[2 * odd + r : P : 32, :].bitcast(I32), dk_s_dealt[16 * odd + r : P : 32, :].bitcast(I32))
-        x2 = sb("x2", [P, S], U32)
+        d_plane = deal("d_plane", dk_s[:], U8)
+        for q in range(4):
+            nc.sync.dma_start(d_plane[32 * q + 1 : 32 * q + 4, :].bitcast(I32), d_plane[32 * q + 8 : 32 * q + 32 : 8, :].bitcast(I32))
+        x2_s = sb("x2_s", [P, S], U8)
+        nc.vector.tensor_copy(x2_s[:], xs[:].indirect(l_two[:]))
+        x2 = sb("x2", [P, S], U32, "xs")
         nc.vector.tensor_copy(x2[:], xw[:].bitcast(U32).indirect(l_two[:]))
         dk = sb("dk", [P, S], U32)
         nc.vector.tensor_copy(dk[:], dw[:].bitcast(U32).indirect(l_k1[:]))
         d_codes = deal("d_codes", dk[:], U32)
-        w2_codes = deal("w2_codes", w2w[:].bitcast(U32), U32)
-        w2_plane = deal("w2_plane", w2s[:], U8)
+        w2_codes = deal("w2_codes", w2w[:].bitcast(U32), U32, nc.gpsimd)
+        w2_plane = deal("w2_plane", w2s[:], U8, nc.gpsimd)
+
+        b_banks = []
+        for t in range(PACK):
+            bank = psum.tile([P, S], F32, name="b%d" % t, tag="side%d" % t)
+            b_banks.append(bank)
+            nc.tensor.matmul_mx(
+                out=bank[:], lhsT=d_codes[:, block(t)].bitcast(FP8X4), lhsT_scale=d_plane[:, block(t)],
+                rhs=x2[:].bitcast(FP8X4), rhs_scale=x2_s[:], start=True, stop=True,
+            )
 
         z_codes = sb("z_codes", [P, S], U32)
         z_plane = sb("z_plane", [P, S], U8)
@@ -167,19 +173,15 @@ def tile_picked_cdjointriebgate_none_po_kernel(
 
         def rows_of_a(h):
             for t in range(PACK):
-                nc.scalar.copy(a_rows[t][:, half_cols(h)], a_banks[h, t // 2][:, t % 2, :])
+                copy = nc.vector.tensor_copy if (h, t // 2) == (1, 1) else nc.scalar.copy
+                copy(a_rows[t][:, half_cols(h)], a_banks[h, t // 2][:, t % 2, :])
 
         gate_half(0)
         gate_half(1)
 
         b_rows = [sb("b_rows%d" % t, [P, S], F32) for t in range(PACK)]
         for t in range(PACK):
-            bank = psum.tile([P, S], F32, name="b%d" % t, tag="side%d" % t)
-            nc.tensor.matmul_mx(
-                out=bank[:], lhsT=d_codes[:, block(t)].bitcast(FP8X4), lhsT_scale=d_plane[:, block(t)],
-                rhs=x2[:].bitcast(FP8X4), rhs_scale=x2_s[:], start=True, stop=True,
-            )
-            nc.scalar.copy(b_rows[t][:], bank[:])
+            nc.scalar.copy(b_rows[t][:], b_banks[t][:])
 
         o_codes = sb("o_codes", [P, S], U32)
         o_plane = sb("o_plane", [P, S], U8)
@@ -210,31 +212,38 @@ def tile_picked_cdjointriebgate_none_po_kernel(
                 nc.tensor.transpose(gate[:, k, :], turned[:, k, :], ident[:])
             return gate
 
-        fetched = {(h, pair): fetch_b(h, pair) for h in range(2) for pair in range(2)}
         rows_of_a(0)
         rows_of_a(1)
-        for h in range(2):
-            res = sb("res%d" % h, [P, PACK, HALF], F32)
-            gates = [gate_of_b(h, pair, fetched[h, pair]) for pair in range(2)]
+        fetched = {(h, pair): fetch_b(h, pair) for h in range(2) for pair in range(2)}
+        def finish(h, first, width, gates):
+            start = h * HALF + first
+            cols = slice(start, start + width)
+            in_half = slice(first, first + width)
+            res = sb("res%d" % start, [P, PACK, width], F32)
             for pair in range(2):
-                ga = sb("ga%d%d" % (h, pair), [P, 2, HALF], F32)
+                ga = sb("ga%d_%d" % (start, pair), [P, 2, width], F32)
                 for i in range(2):
-                    nc.scalar.activation(ga[:, i, :], a_rows[2 * pair + i][:].indirect(half_list(l_n2, h)), ACT.Copy)
-                both = sb("both%d%d" % (h, pair), [P, 2, HALF], F32)
-                nc.vector.tensor_tensor(both[:], a_banks[h, pair][:], ga[:], ADD)
-                nc.vector.tensor_tensor(
-                    res[:, 2 * pair : 2 * pair + 2, :].rearrange("p i c -> p (i c)"), both[:].rearrange("p i c -> p (i c)"),
-                    gates[pair][:].rearrange("p k c -> p (k c)"), MULT,
-                )
-                nc.sync.dma_start(out_rows[:, 2 * pair : 2 * pair + 2, half_cols(h)], res[:, 2 * pair : 2 * pair + 2, :])
-            woven = sb("ow%d" % h, [P, HALF, PACK], BF16)
+                    window = a_rows[2 * pair + i][:].indirect(l_n2[:, start // 16 : (start + width) // 16])
+                    nc.scalar.activation(ga[:, i, :], window, ACT.Copy)
+                both = sb("both%d_%d" % (start, pair), [P, 2, width], F32)
+                nc.vector.tensor_tensor(both[:], a_banks[h, pair][:, :, in_half], ga[:], ADD)
+                gate = gates[pair][:].rearrange("p (i jb) c -> p i (jb c)", i=2)
+                nc.vector.tensor_tensor(res[:, 2 * pair : 2 * pair + 2, :], both[:], gate[:, :, in_half], MULT)
+                nc.sync.dma_start(out_rows[:, 2 * pair : 2 * pair + 2, cols], res[:, 2 * pair : 2 * pair + 2, :])
+            woven = sb("ow%d" % start, [P, width, PACK], BF16)
             nc.vector.tensor_copy(
                 out=woven[:].rearrange("p (c i) t -> p c t i", i=4), in_=res[:].rearrange("p t (c i) -> p c t i", i=4),
             )
             nc.vector.quantize_mx(
-                out=o_codes[:, half_cols(h)].bitcast(FP8X4), scales=o_plane[:, half_cols(h)], in_=woven[:].rearrange("p c t -> p (c t)"),
+                out=o_codes[:, cols].bitcast(FP8X4), scales=o_plane[:, cols], in_=woven[:].rearrange("p c t -> p (c t)"),
             )
-            nc.sync.dma_start(words_of(out_1)[:, half_cols(h)], o_codes[:, half_cols(h)].bitcast(I32))
+            nc.sync.dma_start(words_of(out_1)[:, cols], o_codes[:, cols].bitcast(I32))
+
+        gates = [gate_of_b(0, pair, fetched[0, pair]) for pair in range(2)]
+        finish(0, 0, HALF, gates)
+        gates = [gate_of_b(1, pair, fetched[1, pair]) for pair in range(2)]
+        finish(1, 0, P, gates)
+        finish(1, P, P, gates)
         for q in range(4):
             queue = nc.scalar if q % 2 else nc.sync
             queue.dma_start(out_2[0, 4 * q : 4 * q + 4, :].bitcast(I32), o_plane[32 * q : 32 * q + 4, :].bitcast(I32))

from contextlib import ExitStack

import concourse.mybir as mybir
from concourse.masks import make_identity

F32 = mybir.dt.float32
BF16 = mybir.dt.bfloat16
I32 = mybir.dt.int32
U32 = mybir.dt.uint32
U16 = mybir.dt.uint16
U8 = mybir.dt.uint8
FP8X4 = mybir.dt.float8_e4m3fn_x4
ACT = mybir.ActivationFunctionType
MULT = mybir.AluOpType.mult
ADD = mybir.AluOpType.add

P = 128
PACK = 4
T = 2048
S = 512
HALF = S // 2
LIST_COLS = S // 16
FLOPS = 3 * 2 * 512 * 512 * 512


def tile_picked_cdjointriebgate_none_po_kernel(
    tc, x_words, x_scales, w1_words, w1_scales, gn, w2_words, w2_scales, d_words, d_scales,
    offs, n1, two, k1, n2, n3, out_0, out_1, out_2,
):
    nc = tc.nc

    def words_of(dram):
        return dram[0].rearrange("p n r -> p (n r)").bitcast(I32)

    def half_cols(h):
        return slice(h * HALF, (h + 1) * HALF)

    def half_list(lst, h):
        return lst[:, h * LIST_COLS // 2 : (h + 1) * LIST_COLS // 2]

    def block(t):
        return slice(t * P, (t + 1) * P)

    with ExitStack() as ctx:
        keep = ctx.enter_context(tc.tile_pool(name="keep", bufs=1))
        turns = ctx.enter_context(tc.tile_pool(name="turns", bufs=1))
        psum = ctx.enter_context(tc.psum_pool(name="psum", bufs=1))

        def sb(name, shape, dtype, tag=None):
            return keep.tile(shape, dtype, name=name, tag=tag or name, align_bytes=64)

        def load_list(name, dram):
            lst = keep.tile([P, LIST_COLS], U16, name=name)
            nc.sync.dma_start(lst[:], dram)
            return lst

        def placed(name, shape, dtype, offset):
            return turns.tile(shape, dtype, name=name, offset=offset, align_bytes=64)

        def load_plane(plane, dram, clear, first_queue=nc.sync):
            clear.memset(plane[:].bitcast(I32), 0)
            for q in range(4):
                queue = nc.sync if q else first_queue
                queue.dma_start(plane[32 * q : 32 * q + 4, :].bitcast(I32), dram[0, 4 * q : 4 * q + 4, :].bitcast(I32))

        def deal(name, src, dtype, engine=nc.vector):
            dst = sb(name, [P, S], dtype)
            engine.tensor_copy(out=dst[:].rearrange("p (t m) -> p t m", t=PACK), in_=src.rearrange("p (m t) -> p t m", t=PACK))
            return dst

        l_offs = load_list("l_offs", offs)
        l_two = load_list("l_two", two)
        l_k1 = load_list("l_k1", k1)
        l_n1 = load_list("l_n1", n1)
        l_n3 = load_list("l_n3", n3)
        l_n2 = load_list("l_n2", n2)
        w1w = placed("w1w", [P, S], I32, 4 * T - 64)
        nc.sync.dma_start(w1w[:], words_of(w1_words))
        xw = sb("xw", [P, T], I32)
        nc.sync.dma_start(xw[:], words_of(x_words))
        w1s = sb("w1s", [P, S], U8)
        load_plane(w1s, w1_scales, nc.gpsimd, nc.gpsimd)
        xs = sb("xs", [P, T], U8, "xs")
        load_plane(xs, x_scales, nc.vector)
        ident = sb("ident", [P, P], F32)
        make_identity(nc, ident[:])
        ds = sb("ds", [P, T], U8)
        nc.vector.memset(ds[:].bitcast(I32), 0)
        nc.sync.dma_start(ds[0:P:8, :].bitcast(I32), d_scales[0].bitcast(I32))

        w1_codes = deal("w1_codes", w1w[:].bitcast(U32), U32)
        dw = placed("dw", [P, T], I32, 0)
        nc.sync.dma_start(dw[:], words_of(d_words))
        gain = placed("gain", [P, PACK], F32, 4 * T)
        nc.sync.dma_start(gain[:], gn.rearrange("(p t) o -> p (t o)", t=PACK))
        w2w = placed("w2w", [P, S], I32, 4 * T + 64 + S)
        nc.sync.dma_start(w2w[:], words_of(w2_words))
        w2s = placed("w2s", [P, S], U8, 4 * T + 64)
        load_plane(w2s, w2_scales, nc.gpsimd)
        w1_plane = deal("w1_plane", w1s[:], U8)
        xq_s = sb("xq_s", [P, S], U8)
        xq = sb("xq", [P, S], U32)
        y_banks = {}
        sig_y = [sb("sig_y%d" % t, [P, S], F32) for t in range(PACK)]
        for h in range(2):
            nc.vector.tensor_copy(xq_s[:, half_cols(h)], xs[:].indirect(half_list(l_offs, h)))
            nc.vector.tensor_copy(xq[:, half_cols(h)], xw[:].bitcast(U32).indirect(half_list(l_offs, h)))
            for pair in range(2):
                bank = psum.tile([P, 2, HALF], F32, name="y%d%d" % (h, pair), tag="main%d%d" % (h, pair))
                y_banks[h, pair] = bank
                for i in range(2):
                    t = 2 * pair + i
                    nc.tensor.matmul_mx(
                        out=bank[:, i, :], lhsT=w1_codes[:, block(t)].bitcast(FP8X4), lhsT_scale=w1_plane[:, block(t)],
                        rhs=xq[:, half_cols(h)].bitcast(FP8X4), rhs_scale=xq_s[:, half_cols(h)], start=True, stop=True,
                    )
                for i in range(2):
                    nc.scalar.activation(sig_y[2 * pair + i][:, half_cols(h)], bank[:, i, :], ACT.Sigmoid)

        dk_s = sb("dk_s", [P, S], U8)
        nc.vector.tensor_copy(dk_s[:], ds[:].indirect(l_k1[:]))
        d_plane = deal("d_plane", dk_s[:], U8)
        for q in range(4):
            nc.sync.dma_start(d_plane[32 * q + 1 : 32 * q + 4, :].bitcast(I32), d_plane[32 * q + 8 : 32 * q + 32 : 8, :].bitcast(I32))
        x2_s = sb("x2_s", [P, S], U8)
        nc.vector.tensor_copy(x2_s[:], xs[:].indirect(l_two[:]))
        x2 = sb("x2", [P, S], U32, "xs")
        nc.vector.tensor_copy(x2[:], xw[:].bitcast(U32).indirect(l_two[:]))
        dk = sb("dk", [P, S], U32)
        nc.vector.tensor_copy(dk[:], dw[:].bitcast(U32).indirect(l_k1[:]))
        d_codes = deal("d_codes", dk[:], U32)
        w2_codes = deal("w2_codes", w2w[:].bitcast(U32), U32, nc.gpsimd)
        w2_plane = deal("w2_plane", w2s[:], U8, nc.gpsimd)

        b_banks = []
        for t in range(PACK):
            bank = psum.tile([P, S], F32, name="b%d" % t, tag="side%d" % t)
            b_banks.append(bank)
            nc.tensor.matmul_mx(
                out=bank[:], lhsT=d_codes[:, block(t)].bitcast(FP8X4), lhsT_scale=d_plane[:, block(t)],
                rhs=x2[:].bitcast(FP8X4), rhs_scale=x2_s[:], start=True, stop=True,
            )

        z_codes = sb("z_codes", [P, S], U32)
        z_plane = sb("z_plane", [P, S], U8)
        a_rows = [sb("a_rows%d" % t, [P, S], F32) for t in range(PACK)]
        a_banks = {}

        def gate_half(h):
            z = sb("z%d" % h, [P, PACK, HALF], BF16)
            for t in range(PACK):
                g = sb("gy%d%d" % (h, t), [P, HALF], F32)
                nc.scalar.activation(g[:], sig_y[t][:].indirect(half_list(l_n1, h)), ACT.Copy)
                nc.vector.scalar_tensor_tensor(
                    out=z[:, t, :], in0=y_banks[h, t // 2][:, t % 2, :], scalar=gain[:, t : t + 1], in1=g[:], op0=MULT, op1=MULT,
                )
            woven = sb("zw%d" % h, [P, HALF, PACK], BF16)
            nc.vector.tensor_copy(
                out=woven[:].rearrange("p (c i) t -> p c t i", i=4), in_=z[:].rearrange("p t (c i) -> p c t i", i=4),
            )
            nc.vector.quantize_mx(
                out=z_codes[:, half_cols(h)].bitcast(FP8X4), scales=z_plane[:, half_cols(h)], in_=woven[:].rearrange("p c t -> p (c t)"),
            )
            for pair in range(2):
                bank = psum.tile([P, 2, HALF], F32, name="a%d%d" % (h, pair), tag="main%d%d" % (h, pair))
                a_banks[h, pair] = bank
                for i in range(2):
                    t = 2 * pair + i
                    nc.tensor.matmul_mx(
                        out=bank[:, i, :], lhsT=w2_codes[:, block(t)].bitcast(FP8X4), lhsT_scale=w2_plane[:, block(t)],
                        rhs=z_codes[:, half_cols(h)].bitcast(FP8X4), rhs_scale=z_plane[:, half_cols(h)], start=True, stop=True,
                    )

        def rows_of_a(h):
            for t in range(PACK):
                copy = nc.vector.tensor_copy if (h, t // 2) == (1, 1) else nc.scalar.copy
                copy(a_rows[t][:, half_cols(h)], a_banks[h, t // 2][:, t % 2, :])

        gate_half(0)
        gate_half(1)

        b_rows = [sb("b_rows%d" % t, [P, S], F32) for t in range(PACK)]
        for t in range(PACK):
            nc.scalar.copy(b_rows[t][:], b_banks[t][:])

        o_codes = sb("o_codes", [P, S], U32)
        o_plane = sb("o_plane", [P, S], U8)
        out_rows = out_0.rearrange("(p t) j -> p t j", t=PACK)

        def fetch_b(h, pair):
            gb = sb("gb%d%d" % (h, pair), [P, 2, HALF], F32)
            for i in range(2):
                window = b_rows[2 * pair + i][:].indirect(half_list(l_n3, h))
                if (h, pair) == (0, 0):
                    nc.scalar.activation(gb[:, i, :], window, ACT.Copy)
                else:
                    nc.vector.tensor_copy(gb[:, i, :], window)
            return gb

        def gate_of_b(h, pair, gb):
            tag = "side%d" % (2 * h + pair)
            total = psum.tile([P, 4, P], F32, name="bsum%d%d" % (h, pair), tag=tag)
            for i in range(2):
                for jb in range(2):
                    cols = slice(h * HALF + jb * P, h * HALF + (jb + 1) * P)
                    nc.tensor.matmul(total[:, 2 * i + jb, :], b_rows[2 * pair + i][:, cols], ident[:], is_transpose=True, start=True, stop=False)
                    nc.tensor.matmul(total[:, 2 * i + jb, :], gb[:, i, block(jb)], ident[:], is_transpose=True, start=False, stop=True)
            turned = sb("turned%d%d" % (h, pair), [P, 4, P], F32)
            nc.scalar.activation(turned[:], total[:], ACT.Sigmoid, scale=0.0625)
            gate = psum.tile([P, 4, P], F32, name="gate%d%d" % (h, pair), tag=tag)
            for k in range(4):
                nc.tensor.transpose(gate[:, k, :], turned[:, k, :], ident[:])
            return gate

        rows_of_a(0)
        rows_of_a(1)
        fetched = {(h, pair): fetch_b(h, pair) for h in range(2) for pair in range(2)}
        def finish(h, first, width, gates):
            start = h * HALF + first
            cols = slice(start, start + width)
            in_half = slice(first, first + width)
            res = sb("res%d" % start, [P, PACK, width], F32)
            for pair in range(2):
                ga = sb("ga%d_%d" % (start, pair), [P, 2, width], F32)
                for i in range(2):
                    window = a_rows[2 * pair + i][:].indirect(l_n2[:, start // 16 : (start + width) // 16])
                    nc.scalar.activation(ga[:, i, :], window, ACT.Copy)
                both = sb("both%d_%d" % (start, pair), [P, 2, width], F32)
                nc.vector.tensor_tensor(both[:], a_banks[h, pair][:, :, in_half], ga[:], ADD)
                gate = gates[pair][:].rearrange("p (i jb) c -> p i (jb c)", i=2)
                nc.vector.tensor_tensor(res[:, 2 * pair : 2 * pair + 2, :], both[:], gate[:, :, in_half], MULT)
                nc.sync.dma_start(out_rows[:, 2 * pair : 2 * pair + 2, cols], res[:, 2 * pair : 2 * pair + 2, :])
            woven = sb("ow%d" % start, [P, width, PACK], BF16)
            nc.vector.tensor_copy(
                out=woven[:].rearrange("p (c i) t -> p c t i", i=4), in_=res[:].rearrange("p t (c i) -> p c t i", i=4),
            )
            nc.vector.quantize_mx(
                out=o_codes[:, cols].bitcast(FP8X4), scales=o_plane[:, cols], in_=woven[:].rearrange("p c t -> p (c t)"),
            )
            nc.sync.dma_start(words_of(out_1)[:, cols], o_codes[:, cols].bitcast(I32))

        gates = [gate_of_b(0, pair, fetched[0, pair]) for pair in range(2)]
        finish(0, 0, HALF, gates)
        gates = [gate_of_b(1, pair, fetched[1, pair]) for pair in range(2)]
        finish(1, 0, P, gates)
        finish(1, P, P, gates)
        for q in range(4):
            queue = nc.scalar if q % 2 else nc.sync
            queue.dma_start(out_2[0, 4 * q : 4 * q + 4, :].bitcast(I32), o_plane[32 * q : 32 * q + 4, :].bitcast(I32))
